import numpy as np
import ml_dtypes


def mxq(x, axis, fmt="e4m3"):
    dtype, down = {"e4m3": (ml_dtypes.float8_e4m3fn, 7), "e5m2": (ml_dtypes.float8_e5m2, 14)}[fmt]
    v = np.moveaxis(np.asarray(x, np.float32).astype(ml_dtypes.bfloat16).astype(np.float64), axis, -1)
    blocks = v.reshape(v.shape[:-1] + (-1, 32))
    amax = np.abs(blocks).max(-1, keepdims=True)
    byte = np.maximum(np.where(amax > 0, np.frexp(amax)[1] - 1 + 127, 0) - down, 1)
    scale = np.exp2(byte - 127.0)
    codes = (blocks / scale).astype(np.float32).astype(dtype).astype(np.float64)
    return np.moveaxis((codes * scale).reshape(v.shape), -1, axis)


WIDE = False


def mx_kscale(k):
    if not WIDE:
        return np.ones(k)
    levels = np.array([10, -10, 5, -5, 0])
    if k % 512:
        return np.exp2(np.random.permutation(np.resize(levels, k // 32))).repeat(32)
    a = np.empty((k // 512, 16))
    for p in range(k // 512):
        a[p, :8] = np.random.permutation(np.resize(levels, 8))
        for g in range(8):
            far = levels[np.abs(levels - a[p, g]) >= 10]
            a[p, g + 8] = far[np.random.randint(len(far))]
    return np.exp2(a.ravel()).repeat(32)


def f64(x):
    return np.asarray(x).astype(np.float64)


def striped(idx):
    return np.tile(idx.reshape(-1, 16).T, (8, 1)).astype(np.uint16)


def unstriped(offs):
    return offs[:16].T.reshape(-1).astype(np.int64)


def striped8(idx):
    return np.concatenate([x.reshape(-1, 16).T for x in idx]).astype(np.uint16)


def runs(offs, k):
    lists = np.stack([offs[16 * r : 16 * r + 16].T.reshape(-1) for r in range(8)]).astype(np.int64)
    return lists[np.arange(k) % 512 // 64]


def pack_weight(w):
    k, n = w.shape
    w = f64(np.asarray(w, np.float32).astype(ml_dtypes.bfloat16)).reshape(k // 32, 32, n)
    amax = np.abs(w).max(1)
    byte = np.clip(np.where(amax > 0, np.frexp(amax)[1] - 1 + 127 - 7, 1), 1, 254)
    scaled = (w * np.exp2(127.0 - byte)[:, None, :]).reshape(k, n).astype(np.float32)
    words = np.ascontiguousarray(scaled.reshape(k // 512, 128, 4, n).transpose(0, 1, 3, 2)).astype(ml_dtypes.float8_e4m3fn).view(np.uint8)
    return words, np.ascontiguousarray(byte.astype(np.uint8).reshape(k // 512, 16, n))


def unpack_weight(words, scales):
    g, p, n, _ = words.shape
    vals = np.ascontiguousarray(words).view(ml_dtypes.float8_e4m3fn).astype(np.float64) * np.repeat(np.exp2(scales.astype(np.float64) - 127.0), 8, axis=1)[..., None]
    return vals.transpose(0, 1, 3, 2).reshape(g * 512, n)


def sigmoid(v):
    return 1.0 / (1.0 + np.exp(-np.maximum(v, -700.0)))

def planes(y):
    n, m = y.shape
    v = y.astype(np.float32).astype(ml_dtypes.bfloat16).astype(np.float64).reshape(n // 32, 32, m)
    top = np.abs(v).max(1)
    byte = np.clip(np.where(top > 0, np.frexp(top)[1] - 1 + 127 - 7, 1), 1, 254)
    codes = (v * np.exp2(127.0 - byte)[:, None, :]).reshape(n, m).astype(np.float32).astype(ml_dtypes.float8_e4m3fn).view(np.uint8)
    words = codes.reshape(n // 512, 128, 4, m).transpose(0, 1, 3, 2)
    return np.ascontiguousarray(words), np.ascontiguousarray(byte.astype(np.uint8).reshape(n // 512, 16, m))


K, T, S, G, H = 512, 2048, 512, 2048, 512


def setup_inputs():
    n = np.random.standard_normal
    s = mx_kscale(K)[:, None]
    packed_xT = pack_weight(n((K, T)) * s)
    packed_dT = pack_weight(n((K, G)) / s)
    return {
        "x_words": packed_xT[0],
        "x_scales": packed_xT[1],
        "d_words": packed_dT[0],
        "d_scales": packed_dT[1],
        "gs": (np.random.uniform(0.5, 1.5, (K, 1)) * s).astype(np.float32),
        "offs": striped(np.random.permutation(T)[:S]),
        "k1": striped8(np.random.randint(0, G, (8, H))),
        "n1": striped8(np.stack([np.random.permutation(S) for _ in range(8)])),
        "n2": striped8(np.stack([np.random.permutation(S) for _ in range(8)])),
        "k2": striped8(np.random.randint(0, G, (8, H))),
    }


def reference(x_words, x_scales, d_words, d_scales, gs, offs, k1, n1, n2, k2):
    d_k2 = unpack_weight(d_words, d_scales)[np.arange(K)[:, None], runs(k2, K)]
    d_k1 = unpack_weight(d_words, d_scales)[np.arange(K)[:, None], runs(k1, K)]
    xq = unpack_weight(x_words, x_scales)[:, unstriped(offs)]
    h = 0.0625 * (d_k1.T @ xq)
    z = f64(gs) * ((h[np.arange(H)[:, None], runs(n1, H)]) * (sigmoid(h[np.arange(H)[:, None], runs(n2, H)])))
    out_0 = 0.0625 * ((d_k2.T @ mxq(z, 0, "e4m3")))
    return (out_0,) + planes(out_0)

@@ -1,0 +1,177 @@
+from contextlib import ExitStack
+
+import concourse.mybir as mybir
+
+F32 = mybir.dt.float32
+BF16 = mybir.dt.bfloat16
+I32 = mybir.dt.int32
+U32 = mybir.dt.uint32
+U16 = mybir.dt.uint16
+U8 = mybir.dt.uint8
+FP8X4 = mybir.dt.float8_e4m3fn_x4
+ACT = mybir.ActivationFunctionType
+MULT = mybir.AluOpType.mult
+ADD = mybir.AluOpType.add
+
+P = 128
+PACK = 4
+K = 512
+S = 512
+TABLE = 2048
+SIXTEENTH = 0.0625
+LOOKUP_WIDTHS = (256, 128, 128)
+OUT_WIDTH = 128
+
+FLOPS = 2 * 2 * K * K * S
+
+
+def tile_picked_pqgate_none_po_kernel(
+    tc, x_words, x_scales, d_words, d_scales, gs, offs, k1, n1, n2, k2, out_0, out_1, out_2
+):
+    nc = tc.nc
+    with ExitStack() as ctx:
+        lists = ctx.enter_context(tc.tile_pool(name="lists", bufs=1))
+        pool = ctx.enter_context(tc.tile_pool(name="pool", bufs=1))
+        psum = ctx.enter_context(tc.psum_pool(name="psum", bufs=1))
+
+        def load_list(source, name):
+            tile = lists.tile([P, S // 16], U16, name=name)
+            nc.sync.dma_start(tile[:], source)
+            return tile
+
+        def load_words(source, name):
+            tile = pool.tile([P, TABLE], U32, name=name, align_bytes=64)
+            nc.sync.dma_start(tile[:].bitcast(I32), source[0].rearrange("p n t -> p (n t)").bitcast(I32))
+            return tile
+
+        def load_scale_rows(source, name, tag):
+            tile = pool.tile([P, TABLE], U8, name=name, tag=tag, align_bytes=64)
+            nc.vector.memset(tile[:].bitcast(I32), 0)
+            nc.scalar.dma_start(tile[0:P:8, :].bitcast(I32), source[0].bitcast(I32))
+            return tile
+
+        def place_scale_rows(queue, picked, name):
+            placed = pool.tile(list(picked.shape), U8, name=name, align_bytes=64)
+            nc.vector.memset(placed[:].bitcast(I32), 0)
+            for r in range(4):
+                queue.dma_start(placed[r:P:32, :].bitcast(I32), picked[8 * r : P : 32, :].bitcast(I32))
+            return placed
+
+        def deal(source, dtype, name):
+            dealt = pool.tile([P, K], dtype, name=name, align_bytes=64)
+            nc.vector.tensor_copy(
+                out=dealt[:].rearrange("p (t m) -> p t m", t=PACK),
+                in_=source.rearrange("p (m t) -> p t m", t=PACK),
+            )
+            return dealt
+
+        k1_list = load_list(k1, "k1_list")
+        offs_list = load_list(offs, "offs_list")
+        d_scale_table = load_scale_rows(d_scales, "d_scale_table", "d_scale_table")
+        x_scale_table = load_scale_rows(x_scales, "x_scale_table", "shared")
+        d_word_table = load_words(d_words, "d_word_table")
+        k2_list = load_list(k2, "k2_list")
+        n2_list = load_list(n2, "n2_list")
+        n1_list = load_list(n1, "n1_list")
+        x_word_table = load_words(x_words, "x_word_table")
+        gain = pool.tile([P, PACK], F32, name="gain")
+        nc.gpsimd.dma_start(gain[:], gs.rearrange("(p t) o -> p (t o)", t=PACK))
+
+        first_scales_picked = pool.tile([P, K + S], U8, name="first_scales_picked", tag="picked_scales", align_bytes=64)
+        nc.vector.tensor_copy(first_scales_picked[:, :K], d_scale_table[:].indirect(k1_list[:]))
+        nc.vector.tensor_copy(first_scales_picked[:, K:], x_scale_table[:].indirect(offs_list[:]))
+        first_scales = place_scale_rows(nc.scalar, first_scales_picked, "first_scales")
+
+        w1_picked = pool.tile([P, K], U32, name="w1_picked", tag="shared", align_bytes=64)
+        nc.vector.tensor_copy(w1_picked[:], d_word_table[:].indirect(k1_list[:]))
+        w1_words = deal(w1_picked[:], U32, "w1_words")
+        x_picked = pool.tile([P, S], U32, name="x_picked", align_bytes=64)
+        nc.vector.tensor_copy(x_picked[:], x_word_table[:].indirect(offs_list[:]))
+        w1_scales = deal(first_scales[:, :K], U8, "w1_scales")
+
+        h = []
+        for t in range(PACK):
+            cols = slice(t * P, (t + 1) * P)
+            bank = psum.tile([P, S], F32, name="h_bank%d" % t)
+            nc.tensor.matmul_mx(
+                out=bank[:],
+                lhsT=w1_words[:, cols].bitcast(FP8X4),
+                lhsT_scale=w1_scales[:, cols],
+                rhs=x_picked[:].bitcast(FP8X4),
+                rhs_scale=first_scales[:, K:],
+                start=True,
+                stop=True,
+            )
+            h_t = pool.tile([P, S], F32, name="h%d" % t)
+            nc.scalar.activation(out=h_t[:], in_=bank[:], func=ACT.Copy, scale=SIXTEENTH)
+            h.append(h_t)
+
+        w2_scales_picked = pool.tile([P, K], U8, name="w2_scales_picked", tag="picked_scales", align_bytes=64)
+        nc.vector.tensor_copy(w2_scales_picked[:], d_scale_table[:].indirect(k2_list[:]))
+        w2_scales_dealt = deal(w2_scales_picked[:], U8, "w2_scales_dealt")
+        w2_scales = place_scale_rows(nc.sync, w2_scales_dealt, "w2_scales")
+        w2_picked = pool.tile([P, K], U32, name="w2_picked", tag="d_scale_table", align_bytes=64)
+        nc.vector.tensor_copy(w2_picked[:], d_word_table[:].indirect(k2_list[:]))
+        w2_words = deal(w2_picked[:], U32, "w2_words")
+
+        gained = []
+        for t in range(PACK):
+            gained_t = pool.tile([P, S], F32, name="gained%d" % t)
+            nc.vector.tensor_scalar(gained_t[:], h[t][:], gain[:, t : t + 1], None, MULT)
+            gained.append(gained_t)
+
+        out_codes = pool.tile([P, S], U32, name="out_codes", align_bytes=64)
+        out_scales = pool.tile([P, S], U8, name="out_scales", align_bytes=64)
+        out_rows = out_0.rearrange("(p t) j -> p t j", t=PACK)
+        out_words = out_1[0].rearrange("p n t -> p (n t)").bitcast(I32)
+
+        start = 0
+        for c, width in enumerate(LOOKUP_WIDTHS):
+            entries = slice(start // 16, (start + width) // 16)
+            z = pool.tile([P, PACK, width], F32, name="z%d" % c)
+            for t in range(PACK):
+                gate = pool.tile([P, width], F32, name="gate%d_%d" % (c, t))
+                nc.scalar.activation(out=gate[:], in_=h[t][:].indirect(n2_list[:, entries]), func=ACT.Sigmoid)
+                nc.vector.tensor_tensor(z[:, t, :], gained[t][:].indirect(n1_list[:, entries]), gate[:], MULT)
+            z_grouped = pool.tile([P, width, PACK], BF16, name="z_grouped%d" % c, align_bytes=64)
+            nc.vector.tensor_copy(out=z_grouped[:], in_=z[:].rearrange("p t j -> p j t"))
+            z_codes = pool.tile([P, width], U32, name="z_codes%d" % c, align_bytes=64)
+            z_scales = pool.tile([P, width], U8, name="z_scales%d" % c, align_bytes=64)
+            nc.vector.quantize_mx(
+                out=z_codes[:].bitcast(FP8X4), scales=z_scales[:], in_=z_grouped[:].rearrange("p j t -> p (j t)")
+            )
+            for sub in range(0, width, OUT_WIDTH):
+                inner = slice(sub, sub + OUT_WIDTH)
+                places = slice(start + sub, start + sub + OUT_WIDTH)
+                b = (start + sub) // OUT_WIDTH
+                bank = psum.tile([P, PACK, OUT_WIDTH], F32, name="out_bank%d" % b)
+                for t in range(PACK):
+                    cols = slice(t * P, (t + 1) * P)
+                    nc.tensor.matmul_mx(
+                        out=bank[:, t, :],
+                        lhsT=w2_words[:, cols].bitcast(FP8X4),
+                        lhsT_scale=w2_scales[:, cols],
+                        rhs=z_codes[:, inner].bitcast(FP8X4),
+                        rhs_scale=z_scales[:, inner],
+                        start=True,
+                        stop=True,
+                    )
+                y_grouped = pool.tile([P, OUT_WIDTH, PACK], BF16, name="y_grouped%d" % b, align_bytes=64)
+                nc.scalar.activation(
+                    out=y_grouped[:], in_=bank[:].rearrange("p t j -> p j t"), func=ACT.Copy, scale=SIXTEENTH
+                )
+                y = pool.tile([P, PACK, OUT_WIDTH], F32, name="y%d" % b)
+                nc.scalar.activation(out=y[:], in_=bank[:], func=ACT.Copy, scale=SIXTEENTH)
+                nc.sync.dma_start(out_rows[:, :, places], y[:])
+                nc.vector.quantize_mx(
+                    out=out_codes[:, places].bitcast(FP8X4),
+                    scales=out_scales[:, places],
+                    in_=y_grouped[:].rearrange("p j t -> p (j t)"),
+                )
+            done = slice(start, start + width)
+            nc.sync.dma_start(out_words[:, done], out_codes[:, done].bitcast(I32))
+            start += width
+
+        for r in range(4):
+            queue = nc.sync if r % 2 else nc.scalar
+            queue.dma_start(out_2[0, r:16:4, :].bitcast(I32), out_scales[r:P:32, :].bitcast(I32))

@@ -40,7 +40,7 @@ def tile_picked_pqgate_none_po_kernel(
             return tile
 
         def load_words(source, name):
-            tile = pool.tile([P, TABLE], U32, name=name, align_bytes=64)
+            tile = pool.tile([P, TABLE], U32, name=name, tag=name, align_bytes=64)
             nc.sync.dma_start(tile[:].bitcast(I32), source[0].rearrange("p n t -> p (n t)").bitcast(I32))
             return tile
 
@@ -57,13 +57,11 @@ def tile_picked_pqgate_none_po_kernel(
                 queue.dma_start(placed[r:P:32, :].bitcast(I32), picked[8 * r : P : 32, :].bitcast(I32))
             return placed
 
-        def deal(source, dtype, name):
-            dealt = pool.tile([P, K], dtype, name=name, align_bytes=64)
+        def deal(dealt, source):
             nc.vector.tensor_copy(
-                out=dealt[:].rearrange("p (t m) -> p t m", t=PACK),
+                out=dealt.rearrange("p (t m) -> p t m", t=PACK),
                 in_=source.rearrange("p (m t) -> p t m", t=PACK),
             )
-            return dealt
 
         k1_list = load_list(k1, "k1_list")
         offs_list = load_list(offs, "offs_list")
@@ -73,21 +71,25 @@ def tile_picked_pqgate_none_po_kernel(
         k2_list = load_list(k2, "k2_list")
         n2_list = load_list(n2, "n2_list")
         n1_list = load_list(n1, "n1_list")
-        x_word_table = load_words(x_words, "x_word_table")
         gain = pool.tile([P, PACK], F32, name="gain")
-        nc.gpsimd.dma_start(gain[:], gs.rearrange("(p t) o -> p (t o)", t=PACK))
+        nc.sync.dma_start(gain[:], gs.rearrange("(p t) o -> p (t o)", t=PACK))
+        x_word_table = load_words(x_words, "x_word_table")
 
-        first_scales_picked = pool.tile([P, K + S], U8, name="first_scales_picked", tag="picked_scales", align_bytes=64)
-        nc.vector.tensor_copy(first_scales_picked[:, :K], d_scale_table[:].indirect(k1_list[:]))
-        nc.vector.tensor_copy(first_scales_picked[:, K:], x_scale_table[:].indirect(offs_list[:]))
-        first_scales = place_scale_rows(nc.scalar, first_scales_picked, "first_scales")
+        w1_scales_picked = pool.tile([P, K], U8, name="w1_scales_picked", align_bytes=64)
+        nc.vector.tensor_copy(w1_scales_picked[:], d_scale_table[:].indirect(k1_list[:]))
+        x_scales_picked = pool.tile([P, S], U8, name="x_scales_picked", align_bytes=64)
+        nc.vector.tensor_copy(x_scales_picked[:], x_scale_table[:].indirect(offs_list[:]))
+        first_scales_joined = pool.tile([P, K + S], U8, name="first_scales_joined", align_bytes=64)
+        deal(first_scales_joined[:, :K], w1_scales_picked[:])
+        nc.vector.tensor_copy(first_scales_joined[:, K:].bitcast(I32), x_scales_picked[:].bitcast(I32))
+        first_scales = place_scale_rows(nc.scalar, first_scales_joined, "first_scales")
 
         w1_picked = pool.tile([P, K], U32, name="w1_picked", tag="shared", align_bytes=64)
         nc.vector.tensor_copy(w1_picked[:], d_word_table[:].indirect(k1_list[:]))
-        w1_words = deal(w1_picked[:], U32, "w1_words")
+        w1_words = pool.tile([P, K], U32, name="w1_words", align_bytes=64)
+        deal(w1_words[:], w1_picked[:])
         x_picked = pool.tile([P, S], U32, name="x_picked", align_bytes=64)
         nc.vector.tensor_copy(x_picked[:], x_word_table[:].indirect(offs_list[:]))
-        w1_scales = deal(first_scales[:, :K], U8, "w1_scales")
 
         h = []
         for t in range(PACK):
@@ -96,7 +98,7 @@ def tile_picked_pqgate_none_po_kernel(
             nc.tensor.matmul_mx(
                 out=bank[:],
                 lhsT=w1_words[:, cols].bitcast(FP8X4),
-                lhsT_scale=w1_scales[:, cols],
+                lhsT_scale=first_scales[:, cols],
                 rhs=x_picked[:].bitcast(FP8X4),
                 rhs_scale=first_scales[:, K:],
                 start=True,
@@ -106,13 +108,15 @@ def tile_picked_pqgate_none_po_kernel(
             nc.scalar.activation(out=h_t[:], in_=bank[:], func=ACT.Copy, scale=SIXTEENTH)
             h.append(h_t)
 
-        w2_scales_picked = pool.tile([P, K], U8, name="w2_scales_picked", tag="picked_scales", align_bytes=64)
+        w2_scales_picked = pool.tile([P, K], U8, name="w2_scales_picked", tag="x_word_table", align_bytes=64)
         nc.vector.tensor_copy(w2_scales_picked[:], d_scale_table[:].indirect(k2_list[:]))
-        w2_scales_dealt = deal(w2_scales_picked[:], U8, "w2_scales_dealt")
+        w2_scales_dealt = pool.tile([P, K], U8, name="w2_scales_dealt", align_bytes=64)
+        deal(w2_scales_dealt[:], w2_scales_picked[:])
         w2_scales = place_scale_rows(nc.sync, w2_scales_dealt, "w2_scales")
         w2_picked = pool.tile([P, K], U32, name="w2_picked", tag="d_scale_table", align_bytes=64)
         nc.vector.tensor_copy(w2_picked[:], d_word_table[:].indirect(k2_list[:]))
-        w2_words = deal(w2_picked[:], U32, "w2_words")
+        w2_words = pool.tile([P, K], U32, name="w2_words", align_bytes=64)
+        deal(w2_words[:], w2_picked[:])
 
         gained = []
         for t in range(PACK):

@@ -19,8 +19,9 @@ K = 512
 S = 512
 TABLE = 2048
 SIXTEENTH = 0.0625
-LOOKUP_WIDTHS = (256, 128, 128)
-OUT_WIDTH = 128
+GATE_WIDTH = 256
+BLOCK_WIDTHS = (256, 128, 128)
+BANK = 512
 
 FLOPS = 2 * 2 * K * K * S
 
@@ -44,136 +45,154 @@ def tile_picked_pqgate_none_po_kernel(
             nc.sync.dma_start(tile[:].bitcast(I32), source[0].rearrange("p n t -> p (n t)").bitcast(I32))
             return tile
 
-        def load_scale_rows(source, name, tag):
-            tile = pool.tile([P, TABLE], U8, name=name, tag=tag, align_bytes=64)
-            nc.vector.memset(tile[:].bitcast(I32), 0)
-            nc.scalar.dma_start(tile[0:P:8, :].bitcast(I32), source[0].bitcast(I32))
-            return tile
-
-        def place_scale_rows(queue, picked, name):
-            placed = pool.tile(list(picked.shape), U8, name=name, align_bytes=64)
-            nc.vector.memset(placed[:].bitcast(I32), 0)
-            for r in range(4):
-                queue.dma_start(placed[r:P:32, :].bitcast(I32), picked[8 * r : P : 32, :].bitcast(I32))
-            return placed
-
-        def deal(dealt, source):
+        def deal(dealt, source, layers, run):
             nc.vector.tensor_copy(
-                out=dealt.rearrange("p (t m) -> p t m", t=PACK),
-                in_=source.rearrange("p (m t) -> p t m", t=PACK),
+                out=dealt.rearrange("p (l t c i) -> p l c t i", l=layers, t=PACK, i=run),
+                in_=source.rearrange("p (l c i t) -> p l c t i", l=layers, t=PACK, i=run),
             )
 
         k1_list = load_list(k1, "k1_list")
-        offs_list = load_list(offs, "offs_list")
-        d_scale_table = load_scale_rows(d_scales, "d_scale_table", "d_scale_table")
-        x_scale_table = load_scale_rows(x_scales, "x_scale_table", "shared")
-        d_word_table = load_words(d_words, "d_word_table")
+        d_scale_table = pool.tile([P, TABLE], U8, name="d_scale_table", align_bytes=64)
+        nc.sync.dma_start(
+            d_scale_table[:].bitcast(I32),
+            d_scales[0].bitcast(I32).unsqueeze(1).broadcast_to([16, 8, TABLE // 4]),
+        )
         k2_list = load_list(k2, "k2_list")
+        offs_list = load_list(offs, "offs_list")
+        x_scale_table = pool.tile([P, TABLE], U8, name="x_scale_table", align_bytes=64)
+        nc.vector.memset(x_scale_table[:].bitcast(I32), 0)
+        nc.scalar.dma_start(x_scale_table[0:P:8, :].bitcast(I32), x_scales[0].bitcast(I32))
+        d_word_table = load_words(d_words, "d_word_table")
         n2_list = load_list(n2, "n2_list")
         n1_list = load_list(n1, "n1_list")
+        x_word_table = load_words(x_words, "x_word_table")
         gain = pool.tile([P, PACK], F32, name="gain")
         nc.sync.dma_start(gain[:], gs.rearrange("(p t) o -> p (t o)", t=PACK))
-        x_word_table = load_words(x_words, "x_word_table")
 
-        w1_scales_picked = pool.tile([P, K], U8, name="w1_scales_picked", align_bytes=64)
-        nc.vector.tensor_copy(w1_scales_picked[:], d_scale_table[:].indirect(k1_list[:]))
-        x_scales_picked = pool.tile([P, S], U8, name="x_scales_picked", align_bytes=64)
-        nc.vector.tensor_copy(x_scales_picked[:], x_scale_table[:].indirect(offs_list[:]))
-        first_scales_joined = pool.tile([P, K + S], U8, name="first_scales_joined", align_bytes=64)
-        deal(first_scales_joined[:, :K], w1_scales_picked[:])
-        nc.vector.tensor_copy(first_scales_joined[:, K:].bitcast(I32), x_scales_picked[:].bitcast(I32))
-        first_scales = place_scale_rows(nc.scalar, first_scales_joined, "first_scales")
+        scales_picked = pool.tile([P, 2 * K + S], U8, name="scales_picked", tag="picked", align_bytes=64)
+        nc.vector.tensor_copy(scales_picked[:, :K], d_scale_table[:].indirect(k1_list[:]))
+        nc.vector.tensor_copy(scales_picked[:, K : 2 * K], d_scale_table[:].indirect(k2_list[:]))
+        nc.vector.tensor_copy(scales_picked[:, 2 * K :], x_scale_table[:].indirect(offs_list[:]))
+        scales = pool.tile([P, 2 * K + S], U8, name="scales", align_bytes=64)
+        deal(scales[:, : 2 * K], scales_picked[:, : 2 * K], 2, 16)
+        nc.vector.tensor_copy(scales[:, 2 * K :].bitcast(I32), scales_picked[:, 2 * K :].bitcast(I32))
+        for r, queue in ((1, nc.scalar), (2, nc.sync), (3, nc.scalar)):
+            queue.dma_start(scales[r:P:32, :].bitcast(I32), scales[8 * r : P : 32, :].bitcast(I32))
+        w1_scales = scales[:, :K]
+        w2_scales = scales[:, K : 2 * K]
+        x_picked_scales = scales[:, 2 * K :]
 
-        w1_picked = pool.tile([P, K], U32, name="w1_picked", tag="shared", align_bytes=64)
+        w1_picked = pool.tile([P, K], U32, name="w1_picked", tag="picked", align_bytes=64)
         nc.vector.tensor_copy(w1_picked[:], d_word_table[:].indirect(k1_list[:]))
-        w1_words = pool.tile([P, K], U32, name="w1_words", align_bytes=64)
-        deal(w1_words[:], w1_picked[:])
         x_picked = pool.tile([P, S], U32, name="x_picked", align_bytes=64)
+        w1_words = pool.tile([P, K], U32, name="w1_words", align_bytes=64)
+        deal(w1_words[:], w1_picked[:], 1, 4)
         nc.vector.tensor_copy(x_picked[:], x_word_table[:].indirect(offs_list[:]))
 
         h = []
+        h_banks = []
         for t in range(PACK):
             cols = slice(t * P, (t + 1) * P)
             bank = psum.tile([P, S], F32, name="h_bank%d" % t)
             nc.tensor.matmul_mx(
                 out=bank[:],
                 lhsT=w1_words[:, cols].bitcast(FP8X4),
-                lhsT_scale=first_scales[:, cols],
+                lhsT_scale=w1_scales[:, cols],
                 rhs=x_picked[:].bitcast(FP8X4),
-                rhs_scale=first_scales[:, K:],
+                rhs_scale=x_picked_scales,
                 start=True,
                 stop=True,
             )
             h_t = pool.tile([P, S], F32, name="h%d" % t)
-            nc.scalar.activation(out=h_t[:], in_=bank[:], func=ACT.Copy, scale=SIXTEENTH)
+            nc.scalar.activation(out=h_t[:], in_=bank[:], func=ACT.Copy if t else ACT.Sigmoid, scale=SIXTEENTH)
             h.append(h_t)
+            h_banks.append(bank)
 
-        w2_scales_picked = pool.tile([P, K], U8, name="w2_scales_picked", tag="x_word_table", align_bytes=64)
-        nc.vector.tensor_copy(w2_scales_picked[:], d_scale_table[:].indirect(k2_list[:]))
-        w2_scales_dealt = pool.tile([P, K], U8, name="w2_scales_dealt", align_bytes=64)
-        deal(w2_scales_dealt[:], w2_scales_picked[:])
-        w2_scales = place_scale_rows(nc.sync, w2_scales_dealt, "w2_scales")
-        w2_picked = pool.tile([P, K], U32, name="w2_picked", tag="d_scale_table", align_bytes=64)
+        w2_picked = pool.tile([P, K], U32, name="w2_picked", tag="x_word_table", align_bytes=64)
         nc.vector.tensor_copy(w2_picked[:], d_word_table[:].indirect(k2_list[:]))
-        w2_words = pool.tile([P, K], U32, name="w2_words", align_bytes=64)
-        deal(w2_words[:], w2_picked[:])
 
         gained = []
         for t in range(PACK):
             gained_t = pool.tile([P, S], F32, name="gained%d" % t)
-            nc.vector.tensor_scalar(gained_t[:], h[t][:], gain[:, t : t + 1], None, MULT)
+            if t:
+                nc.vector.tensor_scalar(gained_t[:], h[t][:], gain[:, t : t + 1], None, MULT)
+            else:
+                nc.vector.tensor_scalar(gained_t[:], h_banks[t][:], gain[:, t : t + 1], SIXTEENTH, MULT, MULT)
             gained.append(gained_t)
+
+        w2_words = pool.tile([P, K], U32, name="w2_words", align_bytes=64)
+        deal(w2_words[:], w2_picked[:], 1, 4)
 
         out_codes = pool.tile([P, S], U32, name="out_codes", align_bytes=64)
         out_scales = pool.tile([P, S], U8, name="out_scales", align_bytes=64)
         out_rows = out_0.rearrange("(p t) j -> p t j", t=PACK)
         out_words = out_1[0].rearrange("p n t -> p (n t)").bitcast(I32)
 
+        gates = {}
         start = 0
-        for c, width in enumerate(LOOKUP_WIDTHS):
+        for c, width in enumerate(BLOCK_WIDTHS):
+            places = slice(start, start + width)
             entries = slice(start // 16, (start + width) // 16)
+            g, within = divmod(start, GATE_WIDTH)
             z = pool.tile([P, PACK, width], F32, name="z%d" % c)
             for t in range(PACK):
-                gate = pool.tile([P, width], F32, name="gate%d_%d" % (c, t))
-                nc.scalar.activation(out=gate[:], in_=h[t][:].indirect(n2_list[:, entries]), func=ACT.Sigmoid)
-                nc.vector.tensor_tensor(z[:, t, :], gained[t][:].indirect(n1_list[:, entries]), gate[:], MULT)
+                if within == 0:
+                    gate = pool.tile([P, GATE_WIDTH], F32, name="gate%d_%d" % (g, t))
+                    gate_entries = slice(start // 16, (start + GATE_WIDTH) // 16)
+                    nc.scalar.activation(
+                        out=gate[:],
+                        in_=h[t][:].indirect(n2_list[:, gate_entries]),
+                        func=ACT.Sigmoid if t else ACT.Copy,
+                    )
+                    gates[t] = gate
+                nc.vector.tensor_tensor(
+                    z[:, t, :], gained[t][:].indirect(n1_list[:, entries]), gates[t][:, within : within + width], MULT
+                )
             z_grouped = pool.tile([P, width, PACK], BF16, name="z_grouped%d" % c, align_bytes=64)
-            nc.vector.tensor_copy(out=z_grouped[:], in_=z[:].rearrange("p t j -> p j t"))
+            nc.vector.tensor_copy(
+                out=z_grouped[:].rearrange("p (c i) t -> p c t i", i=4),
+                in_=z[:].rearrange("p t (c i) -> p c t i", i=4),
+            )
             z_codes = pool.tile([P, width], U32, name="z_codes%d" % c, align_bytes=64)
             z_scales = pool.tile([P, width], U8, name="z_scales%d" % c, align_bytes=64)
             nc.vector.quantize_mx(
                 out=z_codes[:].bitcast(FP8X4), scales=z_scales[:], in_=z_grouped[:].rearrange("p j t -> p (j t)")
             )
-            for sub in range(0, width, OUT_WIDTH):
-                inner = slice(sub, sub + OUT_WIDTH)
-                places = slice(start + sub, start + sub + OUT_WIDTH)
-                b = (start + sub) // OUT_WIDTH
-                bank = psum.tile([P, PACK, OUT_WIDTH], F32, name="out_bank%d" % b)
-                for t in range(PACK):
+            per_bank = BANK // width
+            y = pool.tile([P, PACK, width], F32, name="y%d" % c)
+            y_grouped = pool.tile([P, width, PACK], BF16, name="y_grouped%d" % c, align_bytes=64)
+            for first in range(0, PACK, per_bank):
+                bank = psum.tile([P, per_bank, width], F32, name="out_bank%d_%d" % (c, first))
+                for t in range(first, first + per_bank):
                     cols = slice(t * P, (t + 1) * P)
                     nc.tensor.matmul_mx(
-                        out=bank[:, t, :],
+                        out=bank[:, t - first, :],
                         lhsT=w2_words[:, cols].bitcast(FP8X4),
                         lhsT_scale=w2_scales[:, cols],
-                        rhs=z_codes[:, inner].bitcast(FP8X4),
-                        rhs_scale=z_scales[:, inner],
+                        rhs=z_codes[:].bitcast(FP8X4),
+                        rhs_scale=z_scales[:],
                         start=True,
                         stop=True,
                     )
-                y_grouped = pool.tile([P, OUT_WIDTH, PACK], BF16, name="y_grouped%d" % b, align_bytes=64)
+                if per_bank == PACK:
+                    nc.scalar.activation(
+                        out=y_grouped[:], in_=bank[:].rearrange("p t j -> p j t"), func=ACT.Copy, scale=SIXTEENTH
+                    )
                 nc.scalar.activation(
-                    out=y_grouped[:], in_=bank[:].rearrange("p t j -> p j t"), func=ACT.Copy, scale=SIXTEENTH
+                    out=y[:, first : first + per_bank, :], in_=bank[:], func=ACT.Copy, scale=SIXTEENTH
                 )
-                y = pool.tile([P, PACK, OUT_WIDTH], F32, name="y%d" % b)
-                nc.scalar.activation(out=y[:], in_=bank[:], func=ACT.Copy, scale=SIXTEENTH)
-                nc.sync.dma_start(out_rows[:, :, places], y[:])
-                nc.vector.quantize_mx(
-                    out=out_codes[:, places].bitcast(FP8X4),
-                    scales=out_scales[:, places],
-                    in_=y_grouped[:].rearrange("p j t -> p (j t)"),
+            nc.sync.dma_start(out_rows[:, :, places], y[:])
+            if per_bank < PACK:
+                nc.vector.tensor_copy(
+                    out=y_grouped[:].rearrange("p (c i) t -> p c t i", i=4),
+                    in_=y[:].rearrange("p t (c i) -> p c t i", i=4),
                 )
-            done = slice(start, start + width)
-            nc.sync.dma_start(out_words[:, done], out_codes[:, done].bitcast(I32))
+            nc.vector.quantize_mx(
+                out=out_codes[:, places].bitcast(FP8X4),
+                scales=out_scales[:, places],
+                in_=y_grouped[:].rearrange("p j t -> p (j t)"),
+            )
+            nc.sync.dma_start(out_words[:, places], out_codes[:, places].bitcast(I32))
             start += width
 
         for r in range(4):

@@ -45,48 +45,50 @@ def tile_picked_pqgate_none_po_kernel(
             nc.sync.dma_start(tile[:].bitcast(I32), source[0].rearrange("p n t -> p (n t)").bitcast(I32))
             return tile
 
-        def deal(dealt, source, layers, run):
+        def deal(dealt, source, run):
             nc.vector.tensor_copy(
-                out=dealt.rearrange("p (l t c i) -> p l c t i", l=layers, t=PACK, i=run),
-                in_=source.rearrange("p (l c i t) -> p l c t i", l=layers, t=PACK, i=run),
+                out=dealt.rearrange("p (t c i) -> p c t i", t=PACK, i=run),
+                in_=source.rearrange("p (c i t) -> p c t i", t=PACK, i=run),
             )
 
+        def load_scale_rows(source, name):
+            tile = pool.tile([P, TABLE], U8, name=name, tag=name, align_bytes=64)
+            nc.sync.dma_start(
+                tile[:].bitcast(I32), source[0].bitcast(I32).unsqueeze(1).broadcast_to([16, 8, TABLE // 4])
+            )
+            return tile
+
+        def place_scale_rows(queue, plane):
+            for r in range(1, 4):
+                queue.dma_start(plane[r:P:32, :].bitcast(I32), plane[8 * r : P : 32, :].bitcast(I32))
+
         k1_list = load_list(k1, "k1_list")
-        d_scale_table = pool.tile([P, TABLE], U8, name="d_scale_table", align_bytes=64)
-        nc.sync.dma_start(
-            d_scale_table[:].bitcast(I32),
-            d_scales[0].bitcast(I32).unsqueeze(1).broadcast_to([16, 8, TABLE // 4]),
-        )
-        k2_list = load_list(k2, "k2_list")
+        d_scale_table = load_scale_rows(d_scales, "d_scale_table")
         offs_list = load_list(offs, "offs_list")
-        x_scale_table = pool.tile([P, TABLE], U8, name="x_scale_table", align_bytes=64)
-        nc.vector.memset(x_scale_table[:].bitcast(I32), 0)
-        nc.scalar.dma_start(x_scale_table[0:P:8, :].bitcast(I32), x_scales[0].bitcast(I32))
+        x_scale_table = load_scale_rows(x_scales, "x_scale_table")
         d_word_table = load_words(d_words, "d_word_table")
+        x_word_table = load_words(x_words, "x_word_table")
+        k2_list = load_list(k2, "k2_list")
         n2_list = load_list(n2, "n2_list")
         n1_list = load_list(n1, "n1_list")
-        x_word_table = load_words(x_words, "x_word_table")
         gain = pool.tile([P, PACK], F32, name="gain")
         nc.sync.dma_start(gain[:], gs.rearrange("(p t) o -> p (t o)", t=PACK))
 
-        scales_picked = pool.tile([P, 2 * K + S], U8, name="scales_picked", tag="picked", align_bytes=64)
-        nc.vector.tensor_copy(scales_picked[:, :K], d_scale_table[:].indirect(k1_list[:]))
-        nc.vector.tensor_copy(scales_picked[:, K : 2 * K], d_scale_table[:].indirect(k2_list[:]))
-        nc.vector.tensor_copy(scales_picked[:, 2 * K :], x_scale_table[:].indirect(offs_list[:]))
-        scales = pool.tile([P, 2 * K + S], U8, name="scales", align_bytes=64)
-        deal(scales[:, : 2 * K], scales_picked[:, : 2 * K], 2, 16)
-        nc.vector.tensor_copy(scales[:, 2 * K :].bitcast(I32), scales_picked[:, 2 * K :].bitcast(I32))
-        for r, queue in ((1, nc.scalar), (2, nc.sync), (3, nc.scalar)):
-            queue.dma_start(scales[r:P:32, :].bitcast(I32), scales[8 * r : P : 32, :].bitcast(I32))
-        w1_scales = scales[:, :K]
-        w2_scales = scales[:, K : 2 * K]
-        x_picked_scales = scales[:, 2 * K :]
+        first_scales_picked = pool.tile([P, K + S], U8, name="first_scales_picked", tag="picked", align_bytes=64)
+        nc.vector.tensor_copy(first_scales_picked[:, :K], d_scale_table[:].indirect(k1_list[:]))
+        nc.vector.tensor_copy(first_scales_picked[:, K:], x_scale_table[:].indirect(offs_list[:]))
+        first_scales = pool.tile([P, K + S], U8, name="first_scales", align_bytes=64)
+        deal(first_scales[:, :K], first_scales_picked[:, :K], 16)
+        nc.vector.tensor_copy(first_scales[:, K:].bitcast(I32), first_scales_picked[:, K:].bitcast(I32))
+        place_scale_rows(nc.scalar, first_scales)
+        w1_scales = first_scales[:, :K]
+        x_picked_scales = first_scales[:, K:]
 
         w1_picked = pool.tile([P, K], U32, name="w1_picked", tag="picked", align_bytes=64)
         nc.vector.tensor_copy(w1_picked[:], d_word_table[:].indirect(k1_list[:]))
         x_picked = pool.tile([P, S], U32, name="x_picked", align_bytes=64)
         w1_words = pool.tile([P, K], U32, name="w1_words", align_bytes=64)
-        deal(w1_words[:], w1_picked[:], 1, 4)
+        deal(w1_words[:], w1_picked[:], 4)
         nc.vector.tensor_copy(x_picked[:], x_word_table[:].indirect(offs_list[:]))
 
         h = []
@@ -108,8 +110,13 @@ def tile_picked_pqgate_none_po_kernel(
             h.append(h_t)
             h_banks.append(bank)
 
-        w2_picked = pool.tile([P, K], U32, name="w2_picked", tag="x_word_table", align_bytes=64)
+        w2_scales_picked = pool.tile([P, K], U8, name="w2_scales_picked", tag="x_word_table", align_bytes=64)
+        nc.vector.tensor_copy(w2_scales_picked[:], d_scale_table[:].indirect(k2_list[:]))
+        w2_picked = pool.tile([P, K], U32, name="w2_picked", tag="d_scale_table", align_bytes=64)
         nc.vector.tensor_copy(w2_picked[:], d_word_table[:].indirect(k2_list[:]))
+        w2_scales = pool.tile([P, K], U8, name="w2_scales", align_bytes=64)
+        deal(w2_scales[:], w2_scales_picked[:], 16)
+        place_scale_rows(nc.sync, w2_scales)
 
         gained = []
         for t in range(PACK):
@@ -121,7 +128,7 @@ def tile_picked_pqgate_none_po_kernel(
             gained.append(gained_t)
 
         w2_words = pool.tile([P, K], U32, name="w2_words", align_bytes=64)
-        deal(w2_words[:], w2_picked[:], 1, 4)
+        deal(w2_words[:], w2_picked[:], 4)
 
         out_codes = pool.tile([P, S], U32, name="out_codes", align_bytes=64)
         out_scales = pool.tile([P, S], U8, name="out_scales", align_bytes=64)

@@ -65,14 +65,14 @@ def tile_picked_pqgate_none_po_kernel(
         k1_list = load_list(k1, "k1_list")
         d_scale_table = load_scale_rows(d_scales, "d_scale_table")
         offs_list = load_list(offs, "offs_list")
-        x_scale_table = load_scale_rows(x_scales, "x_scale_table")
+        x_scale_table = pool.tile([P, TABLE], U8, name="x_scale_table", tag="x_scale_table", align_bytes=64)
+        nc.vector.memset(x_scale_table[:].bitcast(I32), 0)
+        nc.scalar.dma_start(x_scale_table[0:P:8, :].bitcast(I32), x_scales[0].bitcast(I32))
         d_word_table = load_words(d_words, "d_word_table")
-        x_word_table = load_words(x_words, "x_word_table")
         k2_list = load_list(k2, "k2_list")
+        x_word_table = load_words(x_words, "x_word_table")
         n2_list = load_list(n2, "n2_list")
         n1_list = load_list(n1, "n1_list")
-        gain = pool.tile([P, PACK], F32, name="gain")
-        nc.sync.dma_start(gain[:], gs.rearrange("(p t) o -> p (t o)", t=PACK))
 
         first_scales_picked = pool.tile([P, K + S], U8, name="first_scales_picked", tag="picked", align_bytes=64)
         nc.vector.tensor_copy(first_scales_picked[:, :K], d_scale_table[:].indirect(k1_list[:]))
@@ -81,6 +81,8 @@ def tile_picked_pqgate_none_po_kernel(
         deal(first_scales[:, :K], first_scales_picked[:, :K], 16)
         nc.vector.tensor_copy(first_scales[:, K:].bitcast(I32), first_scales_picked[:, K:].bitcast(I32))
         place_scale_rows(nc.scalar, first_scales)
+        gain = pool.tile([P, PACK], F32, name="gain", tag="x_scale_table", align_bytes=64)
+        nc.sync.dma_start(gain[:], gs.rearrange("(p t) o -> p (t o)", t=PACK))
         w1_scales = first_scales[:, :K]
         x_picked_scales = first_scales[:, K:]
 

from contextlib import ExitStack

import concourse.mybir as mybir

F32 = mybir.dt.float32
BF16 = mybir.dt.bfloat16
I32 = mybir.dt.int32
U32 = mybir.dt.uint32
U16 = mybir.dt.uint16
U8 = mybir.dt.uint8
FP8X4 = mybir.dt.float8_e4m3fn_x4
ACT = mybir.ActivationFunctionType
MULT = mybir.AluOpType.mult
ADD = mybir.AluOpType.add

P = 128
PACK = 4
K = 512
S = 512
TABLE = 2048
SIXTEENTH = 0.0625
GATE_WIDTH = 256
BLOCK_WIDTHS = (256, 128, 128)
BANK = 512

FLOPS = 2 * 2 * K * K * S


def tile_picked_pqgate_none_po_kernel(
    tc, x_words, x_scales, d_words, d_scales, gs, offs, k1, n1, n2, k2, out_0, out_1, out_2
):
    nc = tc.nc
    with ExitStack() as ctx:
        lists = ctx.enter_context(tc.tile_pool(name="lists", bufs=1))
        pool = ctx.enter_context(tc.tile_pool(name="pool", bufs=1))
        psum = ctx.enter_context(tc.psum_pool(name="psum", bufs=1))

        def load_list(source, name):
            tile = lists.tile([P, S // 16], U16, name=name)
            nc.sync.dma_start(tile[:], source)
            return tile

        def load_words(source, name):
            tile = pool.tile([P, TABLE], U32, name=name, tag=name, align_bytes=64)
            nc.sync.dma_start(tile[:].bitcast(I32), source[0].rearrange("p n t -> p (n t)").bitcast(I32))
            return tile

        def deal(dealt, source, run):
            nc.vector.tensor_copy(
                out=dealt.rearrange("p (t c i) -> p c t i", t=PACK, i=run),
                in_=source.rearrange("p (c i t) -> p c t i", t=PACK, i=run),
            )

        def load_scale_rows(source, name):
            tile = pool.tile([P, TABLE], U8, name=name, tag=name, align_bytes=64)
            nc.sync.dma_start(
                tile[:].bitcast(I32), source[0].bitcast(I32).unsqueeze(1).broadcast_to([16, 8, TABLE // 4])
            )
            return tile

        def place_scale_rows(queue, plane):
            for r in range(1, 4):
                queue.dma_start(plane[r:P:32, :].bitcast(I32), plane[8 * r : P : 32, :].bitcast(I32))

        k1_list = load_list(k1, "k1_list")
        d_scale_table = load_scale_rows(d_scales, "d_scale_table")
        offs_list = load_list(offs, "offs_list")
        x_scale_table = pool.tile([P, TABLE], U8, name="x_scale_table", tag="x_scale_table", align_bytes=64)
        nc.vector.memset(x_scale_table[:].bitcast(I32), 0)
        nc.scalar.dma_start(x_scale_table[0:P:8, :].bitcast(I32), x_scales[0].bitcast(I32))
        d_word_table = load_words(d_words, "d_word_table")
        k2_list = load_list(k2, "k2_list")
        x_word_table = load_words(x_words, "x_word_table")
        n2_list = load_list(n2, "n2_list")
        n1_list = load_list(n1, "n1_list")

        first_scales_picked = pool.tile([P, K + S], U8, name="first_scales_picked", tag="picked", align_bytes=64)
        nc.vector.tensor_copy(first_scales_picked[:, :K], d_scale_table[:].indirect(k1_list[:]))
        nc.vector.tensor_copy(first_scales_picked[:, K:], x_scale_table[:].indirect(offs_list[:]))
        first_scales = pool.tile([P, K + S], U8, name="first_scales", align_bytes=64)
        deal(first_scales[:, :K], first_scales_picked[:, :K], 16)
        nc.vector.tensor_copy(first_scales[:, K:].bitcast(I32), first_scales_picked[:, K:].bitcast(I32))
        place_scale_rows(nc.scalar, first_scales)
        gain = pool.tile([P, PACK], F32, name="gain", tag="x_scale_table", align_bytes=64)
        nc.sync.dma_start(gain[:], gs.rearrange("(p t) o -> p (t o)", t=PACK))
        w1_scales = first_scales[:, :K]
        x_picked_scales = first_scales[:, K:]

        w1_picked = pool.tile([P, K], U32, name="w1_picked", tag="picked", align_bytes=64)
        nc.vector.tensor_copy(w1_picked[:], d_word_table[:].indirect(k1_list[:]))
        x_picked = pool.tile([P, S], U32, name="x_picked", align_bytes=64)
        w1_words = pool.tile([P, K], U32, name="w1_words", align_bytes=64)
        deal(w1_words[:], w1_picked[:], 4)
        nc.vector.tensor_copy(x_picked[:], x_word_table[:].indirect(offs_list[:]))

        h = []
        h_banks = []
        for t in range(PACK):
            cols = slice(t * P, (t + 1) * P)
            bank = psum.tile([P, S], F32, name="h_bank%d" % t)
            nc.tensor.matmul_mx(
                out=bank[:],
                lhsT=w1_words[:, cols].bitcast(FP8X4),
                lhsT_scale=w1_scales[:, cols],
                rhs=x_picked[:].bitcast(FP8X4),
                rhs_scale=x_picked_scales,
                start=True,
                stop=True,
            )
            h_t = pool.tile([P, S], F32, name="h%d" % t)
            nc.scalar.activation(out=h_t[:], in_=bank[:], func=ACT.Copy if t else ACT.Sigmoid, scale=SIXTEENTH)
            h.append(h_t)
            h_banks.append(bank)

        w2_scales_picked = pool.tile([P, K], U8, name="w2_scales_picked", tag="x_word_table", align_bytes=64)
        nc.vector.tensor_copy(w2_scales_picked[:], d_scale_table[:].indirect(k2_list[:]))
        w2_picked = pool.tile([P, K], U32, name="w2_picked", tag="d_scale_table", align_bytes=64)
        nc.vector.tensor_copy(w2_picked[:], d_word_table[:].indirect(k2_list[:]))
        w2_scales = pool.tile([P, K], U8, name="w2_scales", align_bytes=64)
        deal(w2_scales[:], w2_scales_picked[:], 16)
        place_scale_rows(nc.sync, w2_scales)

        gained = []
        for t in range(PACK):
            gained_t = pool.tile([P, S], F32, name="gained%d" % t)
            if t:
                nc.vector.tensor_scalar(gained_t[:], h[t][:], gain[:, t : t + 1], None, MULT)
            else:
                nc.vector.tensor_scalar(gained_t[:], h_banks[t][:], gain[:, t : t + 1], SIXTEENTH, MULT, MULT)
            gained.append(gained_t)

        w2_words = pool.tile([P, K], U32, name="w2_words", align_bytes=64)
        deal(w2_words[:], w2_picked[:], 4)

        out_codes = pool.tile([P, S], U32, name="out_codes", align_bytes=64)
        out_scales = pool.tile([P, S], U8, name="out_scales", align_bytes=64)
        out_rows = out_0.rearrange("(p t) j -> p t j", t=PACK)
        out_words = out_1[0].rearrange("p n t -> p (n t)").bitcast(I32)

        gates = {}
        start = 0
        for c, width in enumerate(BLOCK_WIDTHS):
            places = slice(start, start + width)
            entries = slice(start // 16, (start + width) // 16)
            g, within = divmod(start, GATE_WIDTH)
            z = pool.tile([P, PACK, width], F32, name="z%d" % c)
            for t in range(PACK):
                if within == 0:
                    gate = pool.tile([P, GATE_WIDTH], F32, name="gate%d_%d" % (g, t))
                    gate_entries = slice(start // 16, (start + GATE_WIDTH) // 16)
                    nc.scalar.activation(
                        out=gate[:],
                        in_=h[t][:].indirect(n2_list[:, gate_entries]),
                        func=ACT.Sigmoid if t else ACT.Copy,
                    )
                    gates[t] = gate
                nc.vector.tensor_tensor(
                    z[:, t, :], gained[t][:].indirect(n1_list[:, entries]), gates[t][:, within : within + width], MULT
                )
            z_grouped = pool.tile([P, width, PACK], BF16, name="z_grouped%d" % c, align_bytes=64)
            nc.vector.tensor_copy(
                out=z_grouped[:].rearrange("p (c i) t -> p c t i", i=4),
                in_=z[:].rearrange("p t (c i) -> p c t i", i=4),
            )
            z_codes = pool.tile([P, width], U32, name="z_codes%d" % c, align_bytes=64)
            z_scales = pool.tile([P, width], U8, name="z_scales%d" % c, align_bytes=64)
            nc.vector.quantize_mx(
                out=z_codes[:].bitcast(FP8X4), scales=z_scales[:], in_=z_grouped[:].rearrange("p j t -> p (j t)")
            )
            per_bank = BANK // width
            y = pool.tile([P, PACK, width], F32, name="y%d" % c)
            y_grouped = pool.tile([P, width, PACK], BF16, name="y_grouped%d" % c, align_bytes=64)
            for first in range(0, PACK, per_bank):
                bank = psum.tile([P, per_bank, width], F32, name="out_bank%d_%d" % (c, first))
                for t in range(first, first + per_bank):
                    cols = slice(t * P, (t + 1) * P)
                    nc.tensor.matmul_mx(
                        out=bank[:, t - first, :],
                        lhsT=w2_words[:, cols].bitcast(FP8X4),
                        lhsT_scale=w2_scales[:, cols],
                        rhs=z_codes[:].bitcast(FP8X4),
                        rhs_scale=z_scales[:],
                        start=True,
                        stop=True,
                    )
                if per_bank == PACK:
                    nc.scalar.activation(
                        out=y_grouped[:], in_=bank[:].rearrange("p t j -> p j t"), func=ACT.Copy, scale=SIXTEENTH
                    )
                nc.scalar.activation(
                    out=y[:, first : first + per_bank, :], in_=bank[:], func=ACT.Copy, scale=SIXTEENTH
                )
            nc.sync.dma_start(out_rows[:, :, places], y[:])
            if per_bank < PACK:
                nc.vector.tensor_copy(
                    out=y_grouped[:].rearrange("p (c i) t -> p c t i", i=4),
                    in_=y[:].rearrange("p t (c i) -> p c t i", i=4),
                )
            nc.vector.quantize_mx(
                out=out_codes[:, places].bitcast(FP8X4),
                scales=out_scales[:, places],
                in_=y_grouped[:].rearrange("p j t -> p (j t)"),
            )
            nc.sync.dma_start(out_words[:, places], out_codes[:, places].bitcast(I32))
            start += width

        for r in range(4):
            queue = nc.sync if r % 2 else nc.scalar
            queue.dma_start(out_2[0, r:16:4, :].bitcast(I32), out_scales[r:P:32, :].bitcast(I32))
